import numpy as np
import ml_dtypes


def mxq(x, axis, fmt="e4m3"):
    dtype, down = {"e4m3": (ml_dtypes.float8_e4m3fn, 7), "e5m2": (ml_dtypes.float8_e5m2, 14)}[fmt]
    v = np.moveaxis(np.asarray(x, np.float32).astype(ml_dtypes.bfloat16).astype(np.float64), axis, -1)
    blocks = v.reshape(v.shape[:-1] + (-1, 32))
    amax = np.abs(blocks).max(-1, keepdims=True)
    byte = np.maximum(np.where(amax > 0, np.frexp(amax)[1] - 1 + 127, 0) - down, 1)
    scale = np.exp2(byte - 127.0)
    codes = (blocks / scale).astype(np.float32).astype(dtype).astype(np.float64)
    return np.moveaxis((codes * scale).reshape(v.shape), -1, axis)


WIDE = False


def mx_kscale(k):
    if not WIDE:
        return np.ones(k)
    levels = np.array([10, -10, 5, -5, 0])
    if k % 512:
        return np.exp2(np.random.permutation(np.resize(levels, k // 32))).repeat(32)
    a = np.empty((k // 512, 16))
    for p in range(k // 512):
        a[p, :8] = np.random.permutation(np.resize(levels, 8))
        for g in range(8):
            far = levels[np.abs(levels - a[p, g]) >= 10]
            a[p, g + 8] = far[np.random.randint(len(far))]
    return np.exp2(a.ravel()).repeat(32)


def f64(x):
    return np.asarray(x).astype(np.float64)


def striped(idx):
    return np.tile(np.asarray(idx).reshape(-1, 16).T, (8, 1)).astype(np.uint16)


def unstriped(offs):
    return offs[:16].T.reshape(-1).astype(np.int64)


E2M1 = np.array([0.0, 0.5, 1.0, 1.5, 2.0, 3.0, 4.0, 6.0, -0.0, -0.5, -1.0, -1.5, -2.0, -3.0, -4.0, -6.0])


def pack_weight(w, fmt):
    k, n = w.shape
    w = f64(np.asarray(w, np.float32).astype(ml_dtypes.bfloat16)).reshape(k // 32, 32, n)
    amax = np.abs(w).max(1)
    if fmt == "e4m3":
        byte = np.frexp(amax)[1] - 1 + 127 - 7
    else:
        mant, ex = np.frexp(amax / 6.0)
        byte = np.where(mant > 0.5, ex, ex - 1) + 127
    byte = np.clip(np.where(amax > 0, byte, 1), 1, 254)
    scaled = (w * np.exp2(127.0 - byte)[:, None, :]).reshape(k, n).astype(np.float32)
    by_word = np.ascontiguousarray(scaled.reshape(k // 512, 128, 4, n).transpose(0, 1, 3, 2))
    if fmt == "e4m3":
        words = by_word.astype(ml_dtypes.float8_e4m3fn).view(np.uint8)
    else:
        c = by_word.astype(ml_dtypes.float4_e2m1fn).view(np.uint8) & 0xF
        words = (c[..., 0::2] | (c[..., 1::2] << 4)).reshape(k // 512, 128, 2 * n)
    return np.ascontiguousarray(words), np.ascontiguousarray(byte.astype(np.uint8).reshape(k // 512, 16, n))


def unpack_weight(words, scales, fmt):
    g, _, n = scales.shape
    words = np.ascontiguousarray(words).reshape(g, 128, n, -1)
    if fmt == "e4m3":
        vals = words.view(ml_dtypes.float8_e4m3fn).astype(np.float64)
    else:
        nib = np.empty((g, 128, n, 4), np.uint8)
        nib[..., 0::2] = words & 0xF
        nib[..., 1::2] = words >> 4
        vals = E2M1[nib]
    vals = vals * np.repeat(np.exp2(scales.astype(np.float64) - 127.0), 8, axis=1)[..., None]
    return vals.transpose(0, 1, 3, 2).reshape(g * 512, n)


K, Q, T, J, N = 512, 128, 1024, 256, 256


def setup_inputs():
    n = np.random.standard_normal
    idx = np.random.permutation(T)[:J]
    fk = mx_kscale(K)
    pha = np.random.uniform(0.0, 2.0 * np.pi, (Q, 1))
    phb = np.random.uniform(0.0, 2.0 * np.pi, (Q, 1))
    wp = pack_weight(n((K, N)) * 1 / np.sqrt(K) / fk[:, None], "e2m1")
    return {
        "ra": (0.9 * n((Q, T))).astype(np.float32),
        "ia": (0.9 * n((Q, T))).astype(np.float32),
        "rb": (0.9 * n((Q, T))).astype(np.float32),
        "ib": (0.9 * n((Q, T))).astype(np.float32),
        "ca": (np.cos(pha) * fk[::4, None]).astype(np.float32),
        "na": (-np.sin(pha) * fk[::4, None]).astype(np.float32),
        "sa": (np.sin(pha) * fk[::4, None]).astype(np.float32),
        "cb": (np.cos(phb) * fk[::4, None]).astype(np.float32),
        "nb": (-np.sin(phb) * fk[::4, None]).astype(np.float32),
        "sb": (np.sin(phb) * fk[::4, None]).astype(np.float32),
        "w_words": wp[0],
        "w_scales": wp[1],
        "offs": striped(idx),
    }


def reference(ra, ia, rb, ib, ca, na, sa, cb, nb, sb, w_words, w_scales, offs):
    idx = unstriped(offs)
    wu = unpack_weight(w_words, w_scales, "e2m1")
    v0 = f64(ra)[:, idx] * f64(ca)
    v1 = f64(ia)[:, idx] * f64(na)
    v2 = f64(rb)[:, idx] * f64(cb)
    v3 = f64(ib)[:, idx] * f64(nb)
    zr = np.stack([v0, v1, v2, v3], axis=1).reshape(K, J)
    u0 = f64(ra)[:, idx] * f64(sa)
    u1 = f64(ia)[:, idx] * f64(ca)
    u2 = f64(rb)[:, idx] * f64(sb)
    u3 = f64(ib)[:, idx] * f64(cb)
    zi = np.stack([u0, u1, u2, u3], axis=1).reshape(K, J)
    zrq = mxq(zr, 0, "e4m3")
    p = wu.T @ zrq
    ziq = mxq(zi, 0, "e4m3")
    d = wu.T @ ziq
    y = np.square(p) + np.square(d)
    return y

@@ -1,0 +1,115 @@
+from contextlib import ExitStack
+
+import concourse.mybir as mybir
+
+F32 = mybir.dt.float32
+BF16 = mybir.dt.bfloat16
+I32 = mybir.dt.int32
+U32 = mybir.dt.uint32
+U16 = mybir.dt.uint16
+U8 = mybir.dt.uint8
+FP8X4 = mybir.dt.float8_e4m3fn_x4
+FP4X4 = mybir.dt.float4_e2m1fn_x4
+ACT = mybir.ActivationFunctionType
+ALU = mybir.AluOpType
+
+P = 128
+T = 1024
+J = 256
+N = 256
+PACK = 4
+HALF = J // 2
+FLOPS = 2 * 2 * 512 * N * J
+
+
+def tile_list_beams_kernel(tc, ra, ia, rb, ib, ca, na, sa, cb, nb, sb, w_words, w_scales, offs, out):
+    nc = tc.nc
+    with ExitStack() as ctx:
+        pool = ctx.enter_context(tc.tile_pool(name="sb", bufs=1))
+        psum = ctx.enter_context(tc.psum_pool(name="ps", bufs=1))
+
+        def load(queue, name, src, shape, dtype):
+            t = pool.tile(shape, dtype, name=name, align_bytes=64)
+            queue.dma_start(t[:], src)
+            return t
+
+        ra_t = load(nc.sync, "ra_t", ra, [P, T], F32)
+        offs_t = load(nc.sync, "offs_t", offs, [P, J // 16], U16)
+        ca_t = load(nc.scalar, "ca_t", ca, [P, 1], F32)
+        sa_t = load(nc.scalar, "sa_t", sa, [P, 1], F32)
+        ws_rows = pool.tile([4, 4, N // 4], I32, name="ws_rows", align_bytes=64)
+        nc.scalar.dma_start(ws_rows[:], w_scales[0].rearrange("(q r) n -> r q n", r=4).bitcast(I32))
+        ia_t = load(nc.sync, "ia_t", ia, [P, T], F32)
+        na_t = load(nc.sync, "na_t", na, [P, 1], F32)
+        rb_t = load(nc.sync, "rb_t", rb, [P, T], F32)
+        cb_t = load(nc.sync, "cb_t", cb, [P, 1], F32)
+        nb_t = load(nc.sync, "nb_t", nb, [P, 1], F32)
+        ib_t = load(nc.sync, "ib_t", ib, [P, T], F32)
+        sb_t = load(nc.sync, "sb_t", sb, [P, 1], F32)
+        w_t = pool.tile([P, 2 * N], U8, name="w_t", align_bytes=64)
+        nc.sync.dma_start(w_t[:].bitcast(I32), w_words[0].bitcast(I32))
+
+        ws_t = pool.tile([P, N], U8, name="ws_t", align_bytes=64)
+        nc.vector.memset(ws_t[:].bitcast(I32), 0)
+        for q in range(4):
+            nc.vector.tensor_copy(ws_t[32 * q : 32 * q + 4, :].bitcast(I32), ws_rows[:, q, :])
+
+        zr = pool.tile([P, PACK * J], BF16, name="zr", align_bytes=64)
+        zi = pool.tile([P, PACK * J], BF16, name="zi", align_bytes=64)
+
+        def fetch(z, slot, window, scale, j0, j1):
+            nc.scalar.activation(
+                out=z[:, PACK * j0 + slot : PACK * j1 : PACK],
+                in_=window[:].indirect(offs_t[:, j0 // 16 : j1 // 16]),
+                func=ACT.Copy,
+                scale=scale[:],
+            )
+
+        def product(name, z, j0, j1, accs):
+            width = j1 - j0
+            codes = pool.tile([P, width], U32, name=name + "_codes", align_bytes=64)
+            scales = pool.tile([P, width], U8, name=name + "_scales", align_bytes=64)
+            nc.vector.quantize_mx(out=codes[:].bitcast(FP8X4), scales=scales[:], in_=z[:, PACK * j0 : PACK * j1])
+            for h in range(2):
+                nc.tensor.matmul_mx(
+                    out=accs[h],
+                    lhsT=w_t[:, 2 * P * h : 2 * P * (h + 1)].bitcast(FP4X4),
+                    lhsT_scale=ws_t[:, P * h : P * (h + 1)],
+                    rhs=codes[:].bitcast(FP8X4),
+                    rhs_scale=scales[:],
+                    start=True,
+                    stop=True,
+                )
+
+        p_acc = psum.tile([P, 2, J], F32, name="p_acc")
+        da_acc = psum.tile([P, 2, HALF], F32, name="da_acc")
+        db_acc = [psum.tile([P, HALF], F32, name="db_acc%d" % h) for h in range(2)]
+
+        fetch(zr, 0, ra_t, ca_t, 0, J)
+        fetch(zi, 0, ra_t, sa_t, 0, J)
+        fetch(zr, 1, ia_t, na_t, 0, J)
+        fetch(zi, 1, ia_t, ca_t, 0, J)
+        fetch(zr, 2, rb_t, cb_t, 0, J)
+        fetch(zr, 3, ib_t, nb_t, 0, J)
+        product("p", zr, 0, J, [p_acc[:, h, :] for h in range(2)])
+        fetch(zi, 2, rb_t, sb_t, 0, J)
+        fetch(zi, 3, ib_t, cb_t, 0, HALF)
+        product("da", zi, 0, HALF, [da_acc[:, h, :] for h in range(2)])
+        fetch(zi, 3, ib_t, cb_t, HALF, J)
+        product("db", zi, HALF, J, [db_acc[h][:] for h in range(2)])
+
+        p_sq = pool.tile([P, 2, J], F32, name="p_sq")
+        nc.scalar.activation(out=p_sq[:], in_=p_acc[:], func=ACT.Square)
+        out_v = out.rearrange("(h p) j -> p h j", p=P)
+
+        da_sq = pool.tile([P, 2, HALF], F32, name="da_sq")
+        nc.scalar.activation(out=da_sq[:], in_=da_acc[:], func=ACT.Square)
+        ya = pool.tile([P, 2, HALF], F32, name="ya")
+        nc.vector.tensor_tensor(ya[:], da_sq[:], p_sq[:, :, 0:HALF], ALU.add)
+        nc.sync.dma_start(out_v[:, :, 0:HALF], ya[:])
+        for h in range(2):
+            db_sq = pool.tile([P, HALF], F32, name="db_sq%d" % h)
+            nc.scalar.activation(out=db_sq[:], in_=db_acc[h][:], func=ACT.Square)
+            yb = pool.tile([P, HALF], F32, name="yb%d" % h)
+            nc.vector.tensor_tensor(yb[:], db_sq[:], p_sq[:, h, HALF:J], ALU.add)
+            (nc.sync, nc.scalar)[h].dma_start(out_v[:, h, HALF:J], yb[:])

@@ -33,6 +33,11 @@ def tile_list_beams_kernel(tc, ra, ia, rb, ib, ca, na, sa, cb, nb, sb, w_words, 
             queue.dma_start(t[:], src)
             return t
 
+        warm_in = pool.tile([P, 1], F32, name="warm_in")
+        warm_out = pool.tile([P, 1], F32, name="warm_out")
+        nc.gpsimd.memset(warm_in[:], 1.0)
+        nc.scalar.activation(out=warm_out[:], in_=warm_in[:], func=ACT.Copy, scale=warm_in[:])
+
         ra_t = load(nc.sync, "ra_t", ra, [P, T], F32)
         offs_t = load(nc.sync, "offs_t", offs, [P, J // 16], U16)
         ca_t = load(nc.scalar, "ca_t", ca, [P, 1], F32)

@@ -42,15 +42,15 @@ def tile_list_beams_kernel(tc, ra, ia, rb, ib, ca, na, sa, cb, nb, sb, w_words, 
         offs_t = load(nc.sync, "offs_t", offs, [P, J // 16], U16)
         ca_t = load(nc.scalar, "ca_t", ca, [P, 1], F32)
         sa_t = load(nc.scalar, "sa_t", sa, [P, 1], F32)
-        ws_rows = pool.tile([4, 4, N // 4], I32, name="ws_rows", align_bytes=64)
-        nc.scalar.dma_start(ws_rows[:], w_scales[0].rearrange("(q r) n -> r q n", r=4).bitcast(I32))
         ia_t = load(nc.sync, "ia_t", ia, [P, T], F32)
         na_t = load(nc.sync, "na_t", na, [P, 1], F32)
-        rb_t = load(nc.sync, "rb_t", rb, [P, T], F32)
         cb_t = load(nc.sync, "cb_t", cb, [P, 1], F32)
-        nb_t = load(nc.sync, "nb_t", nb, [P, 1], F32)
-        ib_t = load(nc.sync, "ib_t", ib, [P, T], F32)
+        rb_t = load(nc.sync, "rb_t", rb, [P, T], F32)
         sb_t = load(nc.sync, "sb_t", sb, [P, 1], F32)
+        nb_t = load(nc.sync, "nb_t", nb, [P, 1], F32)
+        ws_rows = pool.tile([4, 4, N // 4], I32, name="ws_rows", align_bytes=64)
+        nc.sync.dma_start(ws_rows[:], w_scales[0].rearrange("(q r) n -> r q n", r=4).bitcast(I32))
+        ib_t = load(nc.sync, "ib_t", ib, [P, T], F32)
         w_t = pool.tile([P, 2 * N], U8, name="w_t", align_bytes=64)
         nc.sync.dma_start(w_t[:].bitcast(I32), w_words[0].bitcast(I32))
 
@@ -86,35 +86,40 @@ def tile_list_beams_kernel(tc, ra, ia, rb, ib, ca, na, sa, cb, nb, sb, w_words, 
                     stop=True,
                 )
 
-        p_acc = psum.tile([P, 2, J], F32, name="p_acc")
+        pa_acc = psum.tile([P, 2, HALF], F32, name="pa_acc")
         da_acc = psum.tile([P, 2, HALF], F32, name="da_acc")
+        pb_acc = psum.tile([P, 2, HALF], F32, name="pb_acc")
         db_acc = [psum.tile([P, HALF], F32, name="db_acc%d" % h) for h in range(2)]
 
         fetch(zr, 0, ra_t, ca_t, 0, J)
         fetch(zi, 0, ra_t, sa_t, 0, J)
-        fetch(zr, 1, ia_t, na_t, 0, J)
         fetch(zi, 1, ia_t, ca_t, 0, J)
+        fetch(zr, 1, ia_t, na_t, 0, J)
         fetch(zr, 2, rb_t, cb_t, 0, J)
-        fetch(zr, 3, ib_t, nb_t, 0, J)
-        product("p", zr, 0, J, [p_acc[:, h, :] for h in range(2)])
         fetch(zi, 2, rb_t, sb_t, 0, J)
+        fetch(zr, 3, ib_t, nb_t, 0, HALF)
+        product("pa", zr, 0, HALF, [pa_acc[:, h, :] for h in range(2)])
         fetch(zi, 3, ib_t, cb_t, 0, HALF)
         product("da", zi, 0, HALF, [da_acc[:, h, :] for h in range(2)])
+        fetch(zr, 3, ib_t, nb_t, HALF, J)
+        product("pb", zr, HALF, J, [pb_acc[:, h, :] for h in range(2)])
         fetch(zi, 3, ib_t, cb_t, HALF, J)
         product("db", zi, HALF, J, [db_acc[h][:] for h in range(2)])
 
-        p_sq = pool.tile([P, 2, J], F32, name="p_sq")
-        nc.scalar.activation(out=p_sq[:], in_=p_acc[:], func=ACT.Square)
-        out_v = out.rearrange("(h p) j -> p h j", p=P)
+        def square(name, acc, shape):
+            sq = pool.tile(shape, F32, name=name)
+            nc.scalar.activation(out=sq[:], in_=acc[:], func=ACT.Square)
+            return sq
 
-        da_sq = pool.tile([P, 2, HALF], F32, name="da_sq")
-        nc.scalar.activation(out=da_sq[:], in_=da_acc[:], func=ACT.Square)
+        out_v = out.rearrange("(h p) j -> p h j", p=P)
+        pa_sq = square("pa_sq", pa_acc, [P, 2, HALF])
+        da_sq = square("da_sq", da_acc, [P, 2, HALF])
         ya = pool.tile([P, 2, HALF], F32, name="ya")
-        nc.vector.tensor_tensor(ya[:], da_sq[:], p_sq[:, :, 0:HALF], ALU.add)
+        nc.vector.tensor_tensor(ya[:], da_sq[:], pa_sq[:], ALU.add)
         nc.sync.dma_start(out_v[:, :, 0:HALF], ya[:])
+        pb_sq = square("pb_sq", pb_acc, [P, 2, HALF])
         for h in range(2):
-            db_sq = pool.tile([P, HALF], F32, name="db_sq%d" % h)
-            nc.scalar.activation(out=db_sq[:], in_=db_acc[h][:], func=ACT.Square)
+            db_sq = square("db_sq%d" % h, db_acc[h], [P, HALF])
             yb = pool.tile([P, HALF], F32, name="yb%d" % h)
-            nc.vector.tensor_tensor(yb[:], db_sq[:], p_sq[:, h, HALF:J], ALU.add)
+            nc.vector.tensor_tensor(yb[:], db_sq[:], pb_sq[:, h, :], ALU.add)
             (nc.sync, nc.scalar)[h].dma_start(out_v[:, h, HALF:J], yb[:])

from contextlib import ExitStack

import concourse.mybir as mybir

F32 = mybir.dt.float32
BF16 = mybir.dt.bfloat16
I32 = mybir.dt.int32
U32 = mybir.dt.uint32
U16 = mybir.dt.uint16
U8 = mybir.dt.uint8
FP8X4 = mybir.dt.float8_e4m3fn_x4
FP4X4 = mybir.dt.float4_e2m1fn_x4
ACT = mybir.ActivationFunctionType
ALU = mybir.AluOpType

P = 128
T = 1024
J = 256
N = 256
PACK = 4
HALF = J // 2
FLOPS = 2 * 2 * 512 * N * J


def tile_list_beams_kernel(tc, ra, ia, rb, ib, ca, na, sa, cb, nb, sb, w_words, w_scales, offs, out):
    nc = tc.nc
    with ExitStack() as ctx:
        pool = ctx.enter_context(tc.tile_pool(name="sb", bufs=1))
        psum = ctx.enter_context(tc.psum_pool(name="ps", bufs=1))

        def load(queue, name, src, shape, dtype):
            t = pool.tile(shape, dtype, name=name, align_bytes=64)
            queue.dma_start(t[:], src)
            return t

        warm_in = pool.tile([P, 1], F32, name="warm_in")
        warm_out = pool.tile([P, 1], F32, name="warm_out")
        nc.gpsimd.memset(warm_in[:], 1.0)
        nc.scalar.activation(out=warm_out[:], in_=warm_in[:], func=ACT.Copy, scale=warm_in[:])

        ra_t = load(nc.sync, "ra_t", ra, [P, T], F32)
        offs_t = load(nc.sync, "offs_t", offs, [P, J // 16], U16)
        ca_t = load(nc.scalar, "ca_t", ca, [P, 1], F32)
        sa_t = load(nc.scalar, "sa_t", sa, [P, 1], F32)
        ia_t = load(nc.sync, "ia_t", ia, [P, T], F32)
        na_t = load(nc.sync, "na_t", na, [P, 1], F32)
        cb_t = load(nc.sync, "cb_t", cb, [P, 1], F32)
        rb_t = load(nc.sync, "rb_t", rb, [P, T], F32)
        sb_t = load(nc.sync, "sb_t", sb, [P, 1], F32)
        nb_t = load(nc.sync, "nb_t", nb, [P, 1], F32)
        ws_rows = pool.tile([4, 4, N // 4], I32, name="ws_rows", align_bytes=64)
        nc.sync.dma_start(ws_rows[:], w_scales[0].rearrange("(q r) n -> r q n", r=4).bitcast(I32))
        ib_t = load(nc.sync, "ib_t", ib, [P, T], F32)
        w_t = pool.tile([P, 2 * N], U8, name="w_t", align_bytes=64)
        nc.sync.dma_start(w_t[:].bitcast(I32), w_words[0].bitcast(I32))

        ws_t = pool.tile([P, N], U8, name="ws_t", align_bytes=64)
        nc.vector.memset(ws_t[:].bitcast(I32), 0)
        for q in range(4):
            nc.vector.tensor_copy(ws_t[32 * q : 32 * q + 4, :].bitcast(I32), ws_rows[:, q, :])

        zr = pool.tile([P, PACK * J], BF16, name="zr", align_bytes=64)
        zi = pool.tile([P, PACK * J], BF16, name="zi", align_bytes=64)

        def fetch(z, slot, window, scale, j0, j1):
            nc.scalar.activation(
                out=z[:, PACK * j0 + slot : PACK * j1 : PACK],
                in_=window[:].indirect(offs_t[:, j0 // 16 : j1 // 16]),
                func=ACT.Copy,
                scale=scale[:],
            )

        def product(name, z, j0, j1, accs):
            width = j1 - j0
            codes = pool.tile([P, width], U32, name=name + "_codes", align_bytes=64)
            scales = pool.tile([P, width], U8, name=name + "_scales", align_bytes=64)
            nc.vector.quantize_mx(out=codes[:].bitcast(FP8X4), scales=scales[:], in_=z[:, PACK * j0 : PACK * j1])
            for h in range(2):
                nc.tensor.matmul_mx(
                    out=accs[h],
                    lhsT=w_t[:, 2 * P * h : 2 * P * (h + 1)].bitcast(FP4X4),
                    lhsT_scale=ws_t[:, P * h : P * (h + 1)],
                    rhs=codes[:].bitcast(FP8X4),
                    rhs_scale=scales[:],
                    start=True,
                    stop=True,
                )

        pa_acc = psum.tile([P, 2, HALF], F32, name="pa_acc")
        da_acc = psum.tile([P, 2, HALF], F32, name="da_acc")
        pb_acc = psum.tile([P, 2, HALF], F32, name="pb_acc")
        db_acc = [psum.tile([P, HALF], F32, name="db_acc%d" % h) for h in range(2)]

        fetch(zr, 0, ra_t, ca_t, 0, J)
        fetch(zi, 0, ra_t, sa_t, 0, J)
        fetch(zi, 1, ia_t, ca_t, 0, J)
        fetch(zr, 1, ia_t, na_t, 0, J)
        fetch(zr, 2, rb_t, cb_t, 0, J)
        fetch(zi, 2, rb_t, sb_t, 0, J)
        fetch(zr, 3, ib_t, nb_t, 0, HALF)
        product("pa", zr, 0, HALF, [pa_acc[:, h, :] for h in range(2)])
        fetch(zi, 3, ib_t, cb_t, 0, HALF)
        product("da", zi, 0, HALF, [da_acc[:, h, :] for h in range(2)])
        fetch(zr, 3, ib_t, nb_t, HALF, J)
        product("pb", zr, HALF, J, [pb_acc[:, h, :] for h in range(2)])
        fetch(zi, 3, ib_t, cb_t, HALF, J)
        product("db", zi, HALF, J, [db_acc[h][:] for h in range(2)])

        def square(name, acc, shape):
            sq = pool.tile(shape, F32, name=name)
            nc.scalar.activation(out=sq[:], in_=acc[:], func=ACT.Square)
            return sq

        out_v = out.rearrange("(h p) j -> p h j", p=P)
        pa_sq = square("pa_sq", pa_acc, [P, 2, HALF])
        da_sq = square("da_sq", da_acc, [P, 2, HALF])
        ya = pool.tile([P, 2, HALF], F32, name="ya")
        nc.vector.tensor_tensor(ya[:], da_sq[:], pa_sq[:], ALU.add)
        nc.sync.dma_start(out_v[:, :, 0:HALF], ya[:])
        pb_sq = square("pb_sq", pb_acc, [P, 2, HALF])
        for h in range(2):
            db_sq = square("db_sq%d" % h, db_acc[h], [P, HALF])
            yb = pool.tile([P, HALF], F32, name="yb%d" % h)
            nc.vector.tensor_tensor(yb[:], db_sq[:], pb_sq[:, h, :], ALU.add)
            (nc.sync, nc.scalar)[h].dma_start(out_v[:, h, HALF:J], yb[:])
